import numpy as np
import ml_dtypes


def mxq(x, axis, fmt="e4m3"):
    dtype, down = {"e4m3": (ml_dtypes.float8_e4m3fn, 7), "e5m2": (ml_dtypes.float8_e5m2, 14)}[fmt]
    v = np.moveaxis(np.asarray(x, np.float32).astype(ml_dtypes.bfloat16).astype(np.float64), axis, -1)
    blocks = v.reshape(v.shape[:-1] + (-1, 32))
    amax = np.abs(blocks).max(-1, keepdims=True)
    byte = np.maximum(np.where(amax > 0, np.frexp(amax)[1] - 1 + 127, 0) - down, 1)
    scale = np.exp2(byte - 127.0)
    codes = (blocks / scale).astype(np.float32).astype(dtype).astype(np.float64)
    return np.moveaxis((codes * scale).reshape(v.shape), -1, axis)


WIDE = False


def mx_kscale(k):
    if not WIDE:
        return np.ones(k)
    levels = np.array([10, -10, 5, -5, 0])
    if k % 512:
        return np.exp2(np.random.permutation(np.resize(levels, k // 32))).repeat(32)
    a = np.empty((k // 512, 16))
    for p in range(k // 512):
        a[p, :8] = np.random.permutation(np.resize(levels, 8))
        for g in range(8):
            far = levels[np.abs(levels - a[p, g]) >= 10]
            a[p, g + 8] = far[np.random.randint(len(far))]
    return np.exp2(a.ravel()).repeat(32)


def f64(x):
    return np.asarray(x).astype(np.float64)


def striped(idx):
    return np.tile(idx.reshape(-1, 16).T, (8, 1)).astype(np.uint16)


def unstriped(offs):
    return offs[:16].T.reshape(-1).astype(np.int64)


def striped8(idx):
    return np.concatenate([x.reshape(-1, 16).T for x in idx]).astype(np.uint16)


def runs(offs, k):
    lists = np.stack([offs[16 * r : 16 * r + 16].T.reshape(-1) for r in range(8)]).astype(np.int64)
    return lists[np.arange(k) % 512 // 64]


def pack_weight(w):
    k, n = w.shape
    w = f64(np.asarray(w, np.float32).astype(ml_dtypes.bfloat16)).reshape(k // 32, 32, n)
    amax = np.abs(w).max(1)
    byte = np.clip(np.where(amax > 0, np.frexp(amax)[1] - 1 + 127 - 7, 1), 1, 254)
    scaled = (w * np.exp2(127.0 - byte)[:, None, :]).reshape(k, n).astype(np.float32)
    words = np.ascontiguousarray(scaled.reshape(k // 512, 128, 4, n).transpose(0, 1, 3, 2)).astype(ml_dtypes.float8_e4m3fn).view(np.uint8)
    return words, np.ascontiguousarray(byte.astype(np.uint8).reshape(k // 512, 16, n))


def unpack_weight(words, scales):
    g, p, n, _ = words.shape
    vals = np.ascontiguousarray(words).view(ml_dtypes.float8_e4m3fn).astype(np.float64) * np.repeat(np.exp2(scales.astype(np.float64) - 127.0), 8, axis=1)[..., None]
    return vals.transpose(0, 1, 3, 2).reshape(g * 512, n)


K, T, S, N, H, G, W = 512, 2048, 512, 512, 512, 2048, 256


def setup_inputs():
    n = np.random.standard_normal
    s = mx_kscale(K)[:, None]
    u = mx_kscale(S)
    packed_xT = pack_weight(n((K, T)) * s)
    packed_dT = pack_weight(n((K, G)) / s)
    perm = np.random.permutation(S)
    return {
        "x_words": packed_xT[0],
        "x_scales": packed_xT[1],
        "w1": (n((K, H)) / np.sqrt(K) / s).astype(np.float32),
        "d_words": packed_dT[0],
        "d_scales": packed_dT[1],
        "gn": (np.random.uniform(0.5, 1.5, (H, 1)) * u[:, None]).astype(np.float32),
        "w2": (n((H, N)) / np.sqrt(H) / u[:, None]).astype(np.float32),
        "offs": striped(np.random.permutation(T)[:S]),
        "k1": striped8(np.random.randint(0, G, (8, H))),
        "two": striped(np.random.permutation(T)[:S]),
        "n1": striped(np.random.permutation(S)),
        "n2": striped(np.random.permutation(S)),
        "n3": striped(np.random.permutation(S)),
        "n4": striped(perm[:W]),
        "n5": striped(perm[W:]),
    }


def reference(x_words, x_scales, w1, d_words, d_scales, gn, w2, offs, k1, two, n1, n2, n3, n4, n5):
    d_k1 = unpack_weight(d_words, d_scales)[np.arange(K)[:, None], runs(k1, K)]
    x_two = unpack_weight(x_words, x_scales)[:, unstriped(two)]
    d = 0.0625 * (d_k1.T @ x_two)
    xq = unpack_weight(x_words, x_scales)[:, unstriped(offs)]
    y = mxq(f64(w1), 0, "e4m3").T @ xq
    z = f64(gn) * (d * (y[:, unstriped(n1)] - y) + 0.5 * (d[:, unstriped(n3)] * (y[:, unstriped(n2)] - y)))
    h = mxq(f64(w2), 0, "e4m3").T @ mxq(z, 0, "e4m3")
    pa = h[:, unstriped(n4)]
    pb = h[:, unstriped(n5)]
    rb = np.maximum(pa, pb)
    ra = pa / (np.abs(pb) + 0.5)
    ds = np.zeros((N, S))
    ds[:, unstriped(n4)] = ra
    out = ds.copy()
    out[:, unstriped(n5)] = rb
    return out

@@ -1,0 +1,251 @@
+from contextlib import ExitStack
+
+import concourse.mybir as mybir
+
+K, T, S, N, H, G, W = 512, 2048, 512, 512, 512, 2048, 256
+FLOPS = 2 * (K * H * S + K * H * S + H * N * S)
+
+F32 = mybir.dt.float32
+BF16 = mybir.dt.bfloat16
+I32 = mybir.dt.int32
+U32 = mybir.dt.uint32
+U16 = mybir.dt.uint16
+U8 = mybir.dt.uint8
+FP8X4 = mybir.dt.float8_e4m3fn_x4
+ALU = mybir.AluOpType
+ACT = mybir.ActivationFunctionType
+
+P = 128
+PACK = 4
+HALF = S // 2
+LANES = 16
+
+
+def tile_picked_twkeyflowbratio_none_p_kernel(
+    tc, x_words, x_scales, w1, d_words, d_scales, gn, w2, offs, k1, two, n1, n2, n3, n4, n5, out
+):
+    nc = tc.nc
+    with ExitStack() as ctx:
+        held = ctx.enter_context(tc.tile_pool(name="held", bufs=1))
+        stage = ctx.enter_context(tc.tile_pool(name="stage", bufs=1))
+        ring = ctx.enter_context(tc.tile_pool(name="ring", bufs=8))
+        psum = ctx.enter_context(tc.psum_pool(name="psum", bufs=8))
+
+        def keep(name, shape, dtype):
+            return held.tile(shape, dtype, name=name, align_bytes=64)
+
+        def load_list(name, src):
+            t = held.tile(list(src.shape), U16, name=name)
+            nc.sync.dma_start(t[:], src)
+            return t
+
+        xs_win = keep("xs_win", [P, T], U8)
+        ds_win = keep("ds_win", [P, G], U8)
+        nc.vector.memset(ds_win[:].bitcast(I32), 0)
+
+        offs_t = load_list("offs_t", offs)
+        two_t = load_list("two_t", two)
+        for r in range(4):
+            nc.sync.dma_start(
+                xs_win[r:P:4, :].bitcast(I32),
+                x_scales[0, r:16:4, :].bitcast(I32).unsqueeze(1).broadcast_to([4, 8, T // 4]),
+            )
+        w1_rows = w1.rearrange("(p j) c -> p j c", j=PACK)
+        w1_raw = []
+        for u in range(2):
+            raw = stage.tile([P, PACK, H // 2], F32, name="w1_raw%d" % u, offset=u * PACK * (H // 2) * 4)
+            nc.sync.dma_start(raw[:], w1_rows[:, :, u * (H // 2) : (u + 1) * (H // 2)])
+            w1_raw.append(raw)
+        k1_t = load_list("k1_t", k1)
+        for e in range(2):
+            nc.sync.dma_start(ds_win[e:P:LANES, :].bitcast(I32), d_scales[0, e:16:2, :].bitcast(I32))
+        xw_win = keep("xw_win", [P, T], U32)
+        nc.sync.dma_start(xw_win[:].bitcast(I32), x_words[0].rearrange("p c r -> p (c r)").bitcast(I32))
+        n1_t = load_list("n1_t", n1)
+        n2_t = load_list("n2_t", n2)
+        dw_win = keep("dw_win", [P, G], U32)
+        nc.sync.dma_start(dw_win[:].bitcast(I32), d_words[0].rearrange("p c r -> p (c r)").bitcast(I32))
+        gain = keep("gain", [P, PACK], F32)
+        nc.sync.dma_start(gain[:], gn.rearrange("(p t) o -> p (t o)", t=PACK))
+        n3_t = load_list("n3_t", n3)
+        n4_t = load_list("n4_t", n4)
+        n5_t = load_list("n5_t", n5)
+
+        def pick(name, window, offsets, dtype):
+            t = keep(name, [P, S], dtype)
+            nc.vector.tensor_copy(t[:], window[:].indirect(offsets[:]))
+            return t
+
+        def deal(name, src, dtype, view):
+            t = keep(name, [P, H], dtype)
+            nc.vector.tensor_copy(
+                t[:].bitcast(view).rearrange("p (t m) -> p m t", t=PACK),
+                src[:].bitcast(view).rearrange("p (m t) -> p m t", t=PACK),
+            )
+            return t
+
+        xq_s = pick("xq_s", xs_win, offs_t, U8)
+        x2_s = pick("x2_s", xs_win, two_t, U8)
+        dk_s_raw = pick("dk_s_raw", ds_win, k1_t, U8)
+        dk_s = deal("dk_s", dk_s_raw, U8, U8)
+        for e in range(2):
+            nc.sync.dma_start(dk_s[2 + e : P : 32, :].bitcast(I32), dk_s[16 + e : P : 32, :].bitcast(I32))
+
+        w1_bf = keep("w1_bf", [P, PACK, P, PACK], BF16)
+        for u in range(2):
+            nc.scalar.copy(
+                w1_bf[:, :, u * (P // 2) : (u + 1) * (P // 2), :].rearrange("p t m j -> p m j t"),
+                w1_raw[u][:].rearrange("p j (m t) -> p m j t", t=PACK),
+            )
+        w2_raw = stage.tile([P, PACK, N], F32, name="w2_raw", offset=0)
+        nc.sync.dma_start(w2_raw[:], w2.rearrange("(p j) c -> p j c", j=PACK))
+        w1_q = keep("w1_q", [P, H], U32)
+        w1_s = keep("w1_s", [P, H], U8)
+        nc.vector.quantize_mx(out=w1_q[:].bitcast(FP8X4), scales=w1_s[:], in_=w1_bf[:].rearrange("p t m j -> p (t m j)"))
+        xq_w = pick("xq_w", xw_win, offs_t, U32)
+
+        def product(lhs_q, lhs_s, t, rhs_q, rhs_s, dst):
+            cols = slice(t * P, (t + 1) * P)
+            nc.tensor.matmul_mx(
+                out=dst, lhsT=lhs_q[:, cols].bitcast(FP8X4), lhsT_scale=lhs_s[:, cols],
+                rhs=rhs_q.bitcast(FP8X4), rhs_scale=rhs_s, start=True, stop=True,
+            )
+
+        y_ps = []
+        for t in range(PACK):
+            bank = psum.tile([P, S], F32, name="bank")
+            product(w1_q, w1_s, t, xq_w[:], xq_s[:], bank[:])
+            y_ps.append(bank)
+
+        x2_w = pick("x2_w", xw_win, two_t, U32)
+        dk_w_raw = pick("dk_w_raw", dw_win, k1_t, U32)
+        dk_w = deal("dk_w", dk_w_raw, U32, I32)
+        d_ps = []
+        for t in range(PACK):
+            bank = psum.tile([P, S], F32, name="bank")
+            product(dk_w, dk_s, t, x2_w[:], x2_s[:], bank[:])
+            d_ps.append(bank)
+
+        y_win = [keep("y_win%d" % t, [P, S], F32) for t in range(PACK)]
+        d_win = [keep("d_win%d" % t, [P, S], F32) for t in range(PACK)]
+        h_win = [keep("h_win%d" % t, [P, S], F32) for t in range(PACK)]
+        h_ps = [psum.tile([P, S], F32, name="bank") for t in range(PACK)]
+        w2_bf = keep("w2_bf", [P, N, PACK], BF16)
+        w2_q = keep("w2_q", [P, N], U32)
+        w2_s = keep("w2_s", [P, N], U8)
+        planes = [keep("planes%d" % half, [P, PACK, HALF], BF16) for half in range(2)]
+
+        def fetch(t, half):
+            lc = slice(half * HALF // LANES, (half + 1) * HALF // LANES)
+            diff = ring.tile([P, 2, HALF], F32, name="diff")
+            nc.scalar.activation(diff[:, 0, :], y_win[t][:].indirect(n1_t[:, lc]), ACT.Copy)
+            nc.scalar.activation(diff[:, 1, :], y_win[t][:].indirect(n2_t[:, lc]), ACT.Copy)
+            return diff
+
+        def mix(t, half, diff):
+            cols = slice(half * HALF, (half + 1) * HALF)
+            lc = slice(half * HALF // LANES, (half + 1) * HALF // LANES)
+            nc.vector.tensor_tensor(
+                diff[:], diff[:], y_win[t][:, cols].unsqueeze(1).broadcast_to([P, 2, HALF]), ALU.subtract
+            )
+            far = ring.tile([P, HALF], F32, name="far")
+            nc.vector.tensor_tensor(far[:], d_win[t][:].indirect(n3_t[:, lc]), diff[:, 1, :], ALU.mult)
+            near = ring.tile([P, HALF], F32, name="near")
+            nc.vector.scalar_tensor_tensor(near[:], diff[:, 0, :], 0.0625, d_win[t][:, cols], ALU.mult, ALU.mult)
+            nc.vector.scalar_tensor_tensor(planes[half][:, t, :], far[:], 0.03125, near[:], ALU.mult, ALU.add)
+
+        def y_out(t):
+            nc.scalar.copy(y_win[t][:], y_ps[t][:])
+
+        def d_out(t):
+            if t < 1:
+                nc.vector.tensor_scalar(d_win[t][:], d_ps[t][:], gain[:, t : t + 1], None, ALU.mult)
+            else:
+                nc.scalar.activation(d_win[t][:], d_ps[t][:], ACT.Copy, scale=gain[:, t : t + 1])
+
+        def w2_round(u):
+            cols = slice(u * (N // 2), (u + 1) * (N // 2))
+            nc.scalar.copy(
+                w2_bf[:, cols, :].rearrange("p (c i) j -> p c j i", i=4),
+                w2_raw[:, :, cols].rearrange("p j (c i) -> p c j i", i=4),
+            )
+
+        def w2_quantise():
+            nc.vector.quantize_mx(out=w2_q[:].bitcast(FP8X4), scales=w2_s[:], in_=w2_bf[:].rearrange("p n j -> p (n j)"))
+
+        z_bf = [keep("z_bf%d" % half, [P, HALF, PACK], BF16) for half in range(2)]
+
+        def weave(half, copy, lo, hi):
+            copy(
+                z_bf[half][:, lo:hi, :].rearrange("p (c i) t -> p c t i", i=4),
+                planes[half][:, :, lo:hi].rearrange("p t (c i) -> p c t i", i=4),
+            )
+
+        def last_product(half, by_vector):
+            cols = slice(half * HALF, (half + 1) * HALF)
+            z_q = keep("z_q%d" % half, [P, HALF], U32)
+            z_s = keep("z_s%d" % half, [P, HALF], U8)
+            nc.vector.quantize_mx(out=z_q[:].bitcast(FP8X4), scales=z_s[:], in_=z_bf[half][:].rearrange("p n t -> p (n t)"))
+            for t in range(PACK):
+                product(w2_q, w2_s, t, z_q[:], z_s[:], h_ps[t][:, cols])
+                if t in by_vector:
+                    nc.vector.tensor_copy(h_win[t][:, cols], h_ps[t][:, cols])
+                else:
+                    nc.scalar.copy(h_win[t][:, cols], h_ps[t][:, cols])
+
+        y_out(0)
+        y_out(1)
+        diff = fetch(0, 0)
+        y_out(2)
+        for t in range(PACK):
+            d_out(t)
+            mix(t, 0, diff)
+            if t == 1:
+                y_out(3)
+            diff = fetch((t + 1) % PACK, (t + 1) // PACK)
+        for t in range(PACK):
+            mix(t, 1, diff)
+            if t + 1 < PACK:
+                diff = fetch(t + 1, 1)
+            if t == 1:
+                w2_round(0)
+                w2_round(1)
+                w2_quantise()
+                weave(0, nc.scalar.copy, 0, HALF)
+            if t == 2:
+                last_product(0, ())
+        weave(1, nc.vector.tensor_copy, 0, 160)
+        weave(1, nc.scalar.copy, 160, HALF)
+        last_product(1, (1, 3))
+
+        res = [keep("res%d" % t, [P, S], F32) for t in range(PACK)]
+        pa = keep("pa", [P, PACK, W], F32)
+        pb = keep("pb", [P, PACK, W], F32)
+        root = keep("root", [P, PACK, W], F32)
+        larger = keep("larger", [P, PACK, W], F32)
+        part = keep("part", [P, PACK, W], F32)
+        pairs = (slice(0, 2), slice(2, 4))
+
+        def size(pair):
+            nc.scalar.activation(root[:, pair, :], pb[:, pair, :], ACT.Abs)
+
+        def inverse_root(pair):
+            nc.scalar.activation(root[:, pair, :], root[:, pair, :], ACT.Abs_reciprocal_sqrt, bias=0.5)
+            nc.vector.tensor_tensor(part[:, pair, :], pa[:, pair, :], root[:, pair, :], ALU.mult)
+
+        for t in range(PACK):
+            nc.vector.tensor_copy(pa[:, t, :], h_win[t][:].indirect(n4_t[:]))
+            if t == 3:
+                size(pairs[0])
+            nc.scalar.activation(pb[:, t, :], h_win[t][:].indirect(n5_t[:]), ACT.Copy)
+        for pair in pairs:
+            nc.vector.tensor_tensor(larger[:, pair, :], pa[:, pair, :], pb[:, pair, :], ALU.max)
+        inverse_root(pairs[0])
+        size(pairs[1])
+        inverse_root(pairs[1])
+        for pair in pairs:
+            for t, other in ((pair.start, pair.start + 1), (pair.start + 1, pair.start)):
+                nc.scalar.activation(res[t][:].indirect(n5_t[:]), larger[:, t, :], ACT.Copy)
+                nc.vector.tensor_tensor(res[other][:].indirect(n4_t[:]), part[:, other, :], root[:, other, :], ALU.mult)
+            for t in (pair.start, pair.start + 1):
+                nc.sync.dma_start(out[t * P : (t + 1) * P, :], res[t][:])

@@ -19,6 +19,9 @@ P = 128
 PACK = 4
 HALF = S // 2
 LANES = 16
+GOT_AT = (10, 14, 11, 15, 12, 15, 12, 15)
+DIFF_AT = (0, 7, 0, 7, 0, 7, 0, 7)
+GAIN_AT = (8, 12, 16, 13)
 
 
 def tile_picked_twkeyflowbratio_none_p_kernel(
@@ -28,11 +31,14 @@ def tile_picked_twkeyflowbratio_none_p_kernel(
     with ExitStack() as ctx:
         held = ctx.enter_context(tc.tile_pool(name="held", bufs=1))
         stage = ctx.enter_context(tc.tile_pool(name="stage", bufs=1))
-        ring = ctx.enter_context(tc.tile_pool(name="ring", bufs=8))
+        work = ctx.enter_context(tc.tile_pool(name="work", bufs=1))
         psum = ctx.enter_context(tc.psum_pool(name="psum", bufs=8))
 
         def keep(name, shape, dtype):
             return held.tile(shape, dtype, name=name, align_bytes=64)
+
+        def placed(name, shape, dtype, at):
+            return work.tile(shape, dtype, name=name, offset=at * 1024, align_bytes=64)
 
         def load_list(name, src):
             t = held.tile(list(src.shape), U16, name=name)
@@ -41,8 +47,10 @@ def tile_picked_twkeyflowbratio_none_p_kernel(
 
         xs_win = keep("xs_win", [P, T], U8)
         ds_win = keep("ds_win", [P, G], U8)
-        nc.vector.memset(ds_win[:].bitcast(I32), 0)
 
+        warm = keep("warm", [P, 8], F32)
+        nc.gpsimd.memset(warm[:], 1.0)
+        nc.scalar.activation(warm[:], warm[:], ACT.Abs_reciprocal_sqrt, bias=0.5)
         offs_t = load_list("offs_t", offs)
         two_t = load_list("two_t", two)
         for r in range(4):
@@ -53,17 +61,20 @@ def tile_picked_twkeyflowbratio_none_p_kernel(
         w1_rows = w1.rearrange("(p j) c -> p j c", j=PACK)
         w1_raw = []
         for u in range(2):
-            raw = stage.tile([P, PACK, H // 2], F32, name="w1_raw%d" % u, offset=u * PACK * (H // 2) * 4)
+            raw = stage.tile([P, PACK, H // 2], F32, name="w1_raw%d" % u, offset=H + u * PACK * (H // 2) * 4)
             nc.sync.dma_start(raw[:], w1_rows[:, :, u * (H // 2) : (u + 1) * (H // 2)])
             w1_raw.append(raw)
         k1_t = load_list("k1_t", k1)
         for e in range(2):
-            nc.sync.dma_start(ds_win[e:P:LANES, :].bitcast(I32), d_scales[0, e:16:2, :].bitcast(I32))
+            nc.sync.dma_start(
+                ds_win[e:P:2, :].bitcast(I32),
+                d_scales[0, e:16:2, :].bitcast(I32).unsqueeze(1).broadcast_to([8, 8, G // 4]),
+            )
         xw_win = keep("xw_win", [P, T], U32)
         nc.sync.dma_start(xw_win[:].bitcast(I32), x_words[0].rearrange("p c r -> p (c r)").bitcast(I32))
         n1_t = load_list("n1_t", n1)
         n2_t = load_list("n2_t", n2)
-        dw_win = keep("dw_win", [P, G], U32)
+        dw_win = placed("dw_win", [P, G], U32, 0)
         nc.sync.dma_start(dw_win[:].bitcast(I32), d_words[0].rearrange("p c r -> p (c r)").bitcast(I32))
         gain = keep("gain", [P, PACK], F32)
         nc.sync.dma_start(gain[:], gn.rearrange("(p t) o -> p (t o)", t=PACK))
@@ -71,8 +82,8 @@ def tile_picked_twkeyflowbratio_none_p_kernel(
         n4_t = load_list("n4_t", n4)
         n5_t = load_list("n5_t", n5)
 
-        def pick(name, window, offsets, dtype):
-            t = keep(name, [P, S], dtype)
+        def pick(name, window, offsets, dtype, at=None):
+            t = keep(name, [P, S], dtype) if at is None else placed(name, [P, S], dtype, at)
             nc.vector.tensor_copy(t[:], window[:].indirect(offsets[:]))
             return t
 
@@ -86,7 +97,8 @@ def tile_picked_twkeyflowbratio_none_p_kernel(
 
         xq_s = pick("xq_s", xs_win, offs_t, U8)
         x2_s = pick("x2_s", xs_win, two_t, U8)
-        dk_s_raw = pick("dk_s_raw", ds_win, k1_t, U8)
+        dk_s_raw = stage.tile([P, H], U8, name="dk_s_raw", offset=0)
+        nc.vector.tensor_copy(dk_s_raw[:], ds_win[:].indirect(k1_t[:]))
         dk_s = deal("dk_s", dk_s_raw, U8, U8)
         for e in range(2):
             nc.sync.dma_start(dk_s[2 + e : P : 32, :].bitcast(I32), dk_s[16 + e : P : 32, :].bitcast(I32))
@@ -126,18 +138,23 @@ def tile_picked_twkeyflowbratio_none_p_kernel(
             product(dk_w, dk_s, t, x2_w[:], x2_s[:], bank[:])
             d_ps.append(bank)
 
-        y_win = [keep("y_win%d" % t, [P, S], F32) for t in range(PACK)]
+        y_win = [placed("y_win2", [P, S], F32, 4) if t == 2 else keep("y_win%d" % t, [P, S], F32) for t in range(PACK)]
         d_win = [keep("d_win%d" % t, [P, S], F32) for t in range(PACK)]
         h_win = [keep("h_win%d" % t, [P, S], F32) for t in range(PACK)]
         h_ps = [psum.tile([P, S], F32, name="bank") for t in range(PACK)]
-        w2_bf = keep("w2_bf", [P, N, PACK], BF16)
         w2_q = keep("w2_q", [P, N], U32)
         w2_s = keep("w2_s", [P, N], U8)
+        gains = []
+        for t in range(PACK):
+            g = work.tile([P, 1], F32, name="gain%d" % t, offset=GAIN_AT[t] * 1024, align_bytes=64)
+            nc.gpsimd.tensor_scalar(g[:], gain[:, t : t + 1], 0.0625, 0.0, ALU.mult, ALU.add)
+            gains.append(g)
         planes = [keep("planes%d" % half, [P, PACK, HALF], BF16) for half in range(2)]
 
         def fetch(t, half):
             lc = slice(half * HALF // LANES, (half + 1) * HALF // LANES)
-            diff = ring.tile([P, 2, HALF], F32, name="diff")
+            unit = half * PACK + t
+            diff = placed("got%d" % unit, [P, 2, HALF], F32, GOT_AT[unit])
             nc.scalar.activation(diff[:, 0, :], y_win[t][:].indirect(n1_t[:, lc]), ACT.Copy)
             nc.scalar.activation(diff[:, 1, :], y_win[t][:].indirect(n2_t[:, lc]), ACT.Copy)
             return diff
@@ -145,33 +162,38 @@ def tile_picked_twkeyflowbratio_none_p_kernel(
         def mix(t, half, diff):
             cols = slice(half * HALF, (half + 1) * HALF)
             lc = slice(half * HALF // LANES, (half + 1) * HALF // LANES)
+            unit = half * PACK + t
+            got = diff
+            diff = placed("diff%d" % unit, [P, 2, HALF], F32, DIFF_AT[unit])
             nc.vector.tensor_tensor(
-                diff[:], diff[:], y_win[t][:, cols].unsqueeze(1).broadcast_to([P, 2, HALF]), ALU.subtract
+                diff[:], got[:], y_win[t][:, cols].unsqueeze(1).broadcast_to([P, 2, HALF]), ALU.subtract
             )
-            far = ring.tile([P, HALF], F32, name="far")
+            far = placed("far%d" % unit, [P, HALF], F32, 20 + 2 * unit)
             nc.vector.tensor_tensor(far[:], d_win[t][:].indirect(n3_t[:, lc]), diff[:, 1, :], ALU.mult)
-            near = ring.tile([P, HALF], F32, name="near")
-            nc.vector.scalar_tensor_tensor(near[:], diff[:, 0, :], 0.0625, d_win[t][:, cols], ALU.mult, ALU.mult)
-            nc.vector.scalar_tensor_tensor(planes[half][:, t, :], far[:], 0.03125, near[:], ALU.mult, ALU.add)
+            near = placed("near%d" % unit, [P, HALF], F32, 21 + 2 * unit)
+            nc.vector.tensor_tensor(near[:], diff[:, 0, :], d_win[t][:, cols], ALU.mult)
+            nc.vector.scalar_tensor_tensor(planes[half][:, t, :], far[:], 0.5, near[:], ALU.mult, ALU.add)
 
         def y_out(t):
-            nc.scalar.copy(y_win[t][:], y_ps[t][:])
+            copy = nc.vector.tensor_copy if t == 2 else nc.scalar.copy
+            copy(y_win[t][:], y_ps[t][:])
 
         def d_out(t):
             if t < 1:
-                nc.vector.tensor_scalar(d_win[t][:], d_ps[t][:], gain[:, t : t + 1], None, ALU.mult)
+                nc.vector.tensor_scalar(d_win[t][:], d_ps[t][:], gains[t][:], None, ALU.mult)
             else:
-                nc.scalar.activation(d_win[t][:], d_ps[t][:], ACT.Copy, scale=gain[:, t : t + 1])
+                nc.scalar.activation(d_win[t][:], d_ps[t][:], ACT.Copy, scale=gains[t][:])
 
         def w2_round(u):
             cols = slice(u * (N // 2), (u + 1) * (N // 2))
+            w2_bf = placed("w2_bf%d" % u, [P, N // 2, PACK], BF16, 20 + 2 * (2 + u))
             nc.scalar.copy(
-                w2_bf[:, cols, :].rearrange("p (c i) j -> p c j i", i=4),
+                w2_bf[:].rearrange("p (c i) j -> p c j i", i=4),
                 w2_raw[:, :, cols].rearrange("p j (c i) -> p c j i", i=4),
             )
-
-        def w2_quantise():
-            nc.vector.quantize_mx(out=w2_q[:].bitcast(FP8X4), scales=w2_s[:], in_=w2_bf[:].rearrange("p n j -> p (n j)"))
+            nc.vector.quantize_mx(
+                out=w2_q[:, cols].bitcast(FP8X4), scales=w2_s[:, cols], in_=w2_bf[:].rearrange("p n j -> p (n j)")
+            )
 
         z_bf = [keep("z_bf%d" % half, [P, HALF, PACK], BF16) for half in range(2)]
 
@@ -195,30 +217,30 @@ def tile_picked_twkeyflowbratio_none_p_kernel(
 
         y_out(0)
         y_out(1)
-        diff = fetch(0, 0)
+        got = [fetch(0, 0)]
         y_out(2)
-        for t in range(PACK):
-            d_out(t)
-            mix(t, 0, diff)
-            if t == 1:
-                y_out(3)
-            diff = fetch((t + 1) % PACK, (t + 1) // PACK)
-        for t in range(PACK):
-            mix(t, 1, diff)
-            if t + 1 < PACK:
-                diff = fetch(t + 1, 1)
-            if t == 1:
+        got.append(fetch(1, 0))
+        y_out(3)
+        for unit in range(2 * PACK):
+            half, t = divmod(unit, PACK)
+            if half == 0:
+                d_out(t)
+            mix(t, half, got[unit])
+            if unit + 2 < 2 * PACK:
+                got.append(fetch((unit + 2) % PACK, (unit + 2) // PACK))
+            if unit == 4:
                 w2_round(0)
+            if unit == 5:
                 w2_round(1)
-                w2_quantise()
                 weave(0, nc.scalar.copy, 0, HALF)
-            if t == 2:
+            if unit == 6:
                 last_product(0, ())
         weave(1, nc.vector.tensor_copy, 0, 160)
         weave(1, nc.scalar.copy, 160, HALF)
         last_product(1, (1, 3))
 
-        res = [keep("res%d" % t, [P, S], F32) for t in range(PACK)]
+        size = [placed("size%d" % u, [P, 2, W], F32, (36, 40)[u]) for u in range(2)]
+        res = [placed("res%d" % t, [P, S], F32, (39, 44, 41, 46)[t]) for t in range(PACK)]
         pa = keep("pa", [P, PACK, W], F32)
         pb = keep("pb", [P, PACK, W], F32)
         root = keep("root", [P, PACK, W], F32)
@@ -226,26 +248,27 @@ def tile_picked_twkeyflowbratio_none_p_kernel(
         part = keep("part", [P, PACK, W], F32)
         pairs = (slice(0, 2), slice(2, 4))
 
-        def size(pair):
-            nc.scalar.activation(root[:, pair, :], pb[:, pair, :], ACT.Abs)
-
-        def inverse_root(pair):
-            nc.scalar.activation(root[:, pair, :], root[:, pair, :], ACT.Abs_reciprocal_sqrt, bias=0.5)
-            nc.vector.tensor_tensor(part[:, pair, :], pa[:, pair, :], root[:, pair, :], ALU.mult)
-
         for t in range(PACK):
             nc.vector.tensor_copy(pa[:, t, :], h_win[t][:].indirect(n4_t[:]))
-            if t == 3:
-                size(pairs[0])
             nc.scalar.activation(pb[:, t, :], h_win[t][:].indirect(n5_t[:]), ACT.Copy)
-        for pair in pairs:
+        for u, pair in enumerate(pairs):
+            nc.scalar.activation(size[u][:], pb[:, pair, :], ACT.Abs)
             nc.vector.tensor_tensor(larger[:, pair, :], pa[:, pair, :], pb[:, pair, :], ALU.max)
-        inverse_root(pairs[0])
-        size(pairs[1])
-        inverse_root(pairs[1])
-        for pair in pairs:
-            for t, other in ((pair.start, pair.start + 1), (pair.start + 1, pair.start)):
-                nc.scalar.activation(res[t][:].indirect(n5_t[:]), larger[:, t, :], ACT.Copy)
-                nc.vector.tensor_tensor(res[other][:].indirect(n4_t[:]), part[:, other, :], root[:, other, :], ALU.mult)
-            for t in (pair.start, pair.start + 1):
-                nc.sync.dma_start(out[t * P : (t + 1) * P, :], res[t][:])
+        for u, pair in enumerate(pairs):
+            nc.scalar.activation(root[:, pair, :], size[u][:], ACT.Abs_reciprocal_sqrt, bias=0.5)
+            nc.vector.tensor_tensor(part[:, pair, :], pa[:, pair, :], root[:, pair, :], ALU.mult)
+
+        def put_larger(t):
+            nc.scalar.activation(res[t][:].indirect(n5_t[:]), larger[:, t, :], ACT.Copy)
+
+        def put_ratio(t):
+            nc.vector.tensor_tensor(res[t][:].indirect(n4_t[:]), part[:, t, :], root[:, t, :], ALU.mult)
+
+        for t in (0, 2):
+            put_larger(t)
+            put_ratio(t + 1)
+        for t in (0, 2):
+            put_larger(t + 1)
+            put_ratio(t)
+            nc.sync.dma_start(out[(t + 1) * P : (t + 2) * P, :], res[t + 1][:])
+            nc.sync.dma_start(out[t * P : (t + 1) * P, :], res[t][:])

@@ -19,9 +19,11 @@ P = 128
 PACK = 4
 HALF = S // 2
 LANES = 16
-GOT_AT = (10, 14, 11, 15, 12, 15, 12, 15)
-DIFF_AT = (0, 7, 0, 7, 0, 7, 0, 7)
-GAIN_AT = (8, 12, 16, 13)
+PARTS = ((0, 384), (384, 512))
+TRIPLE = (3,)
+GOT_AT = (14, 22, 15, 23, 16, 23, 16, 23)
+DIFF_AT = (6, 10)
+GAIN_AT = (10, 17, 25, 18)
 
 
 def tile_picked_twkeyflowbratio_none_p_kernel(
@@ -45,75 +47,81 @@ def tile_picked_twkeyflowbratio_none_p_kernel(
             nc.sync.dma_start(t[:], src)
             return t
 
-        xs_win = keep("xs_win", [P, T], U8)
+        xs_win = placed("xs_win", [P, T], U8, 0)
         ds_win = keep("ds_win", [P, G], U8)
-
+        x_s = keep("x_s", [P, 2 * S], U8)
+        nc.gpsimd.memset(x_s[:].bitcast(I32), 0)
         warm = keep("warm", [P, 8], F32)
         nc.gpsimd.memset(warm[:], 1.0)
         nc.scalar.activation(warm[:], warm[:], ACT.Abs_reciprocal_sqrt, bias=0.5)
+
+        def load_scales(window, scales):
+            nc.sync.dma_start(window[:].bitcast(I32), scales[0].bitcast(I32).unsqueeze(1).broadcast_to([16, 8, T // 4]))
+
         offs_t = load_list("offs_t", offs)
+        nc.sync.dma_start(
+            xs_win[:32, :].bitcast(I32), x_scales[0].bitcast(I32).unsqueeze(1).broadcast_to([16, 2, T // 4])
+        )
+        nc.vector.memset(xs_win[32:64, :].bitcast(I32), 0)
+        nc.vector.memset(xs_win[64:, :].bitcast(I32), 0)
         two_t = load_list("two_t", two)
-        for r in range(4):
-            nc.sync.dma_start(
-                xs_win[r:P:4, :].bitcast(I32),
-                x_scales[0, r:16:4, :].bitcast(I32).unsqueeze(1).broadcast_to([4, 8, T // 4]),
-            )
+        k1_t = load_list("k1_t", k1)
+        load_scales(ds_win, d_scales)
+        n1_t = load_list("n1_t", n1)
+        n2_t = load_list("n2_t", n2)
         w1_rows = w1.rearrange("(p j) c -> p j c", j=PACK)
         w1_raw = []
         for u in range(2):
             raw = stage.tile([P, PACK, H // 2], F32, name="w1_raw%d" % u, offset=H + u * PACK * (H // 2) * 4)
             nc.sync.dma_start(raw[:], w1_rows[:, :, u * (H // 2) : (u + 1) * (H // 2)])
             w1_raw.append(raw)
-        k1_t = load_list("k1_t", k1)
-        for e in range(2):
-            nc.sync.dma_start(
-                ds_win[e:P:2, :].bitcast(I32),
-                d_scales[0, e:16:2, :].bitcast(I32).unsqueeze(1).broadcast_to([8, 8, G // 4]),
-            )
-        xw_win = keep("xw_win", [P, T], U32)
-        nc.sync.dma_start(xw_win[:].bitcast(I32), x_words[0].rearrange("p c r -> p (c r)").bitcast(I32))
-        n1_t = load_list("n1_t", n1)
-        n2_t = load_list("n2_t", n2)
-        dw_win = placed("dw_win", [P, G], U32, 0)
-        nc.sync.dma_start(dw_win[:].bitcast(I32), d_words[0].rearrange("p c r -> p (c r)").bitcast(I32))
-        gain = keep("gain", [P, PACK], F32)
-        nc.sync.dma_start(gain[:], gn.rearrange("(p t) o -> p (t o)", t=PACK))
         n3_t = load_list("n3_t", n3)
         n4_t = load_list("n4_t", n4)
         n5_t = load_list("n5_t", n5)
+        xw_win = keep("xw_win", [P, T], U32)
+        nc.sync.dma_start(xw_win[:].bitcast(I32), x_words[0].rearrange("p c r -> p (c r)").bitcast(I32))
 
-        def pick(name, window, offsets, dtype, at=None):
-            t = keep(name, [P, S], dtype) if at is None else placed(name, [P, S], dtype, at)
+        def pick(name, window, offsets, dtype):
+            t = keep(name, [P, S], dtype)
             nc.vector.tensor_copy(t[:], window[:].indirect(offsets[:]))
             return t
 
-        def deal(name, src, dtype, view):
+        def deal(name, src, dtype, run):
             t = keep(name, [P, H], dtype)
             nc.vector.tensor_copy(
-                t[:].bitcast(view).rearrange("p (t m) -> p m t", t=PACK),
-                src[:].bitcast(view).rearrange("p (m t) -> p m t", t=PACK),
+                t[:].bitcast(I32).rearrange("p (t b u) -> p t b u", t=PACK, u=run),
+                src[:].bitcast(I32).rearrange("p (b t u) -> p t b u", t=PACK, u=run),
             )
             return t
 
-        xq_s = pick("xq_s", xs_win, offs_t, U8)
-        x2_s = pick("x2_s", xs_win, two_t, U8)
+        x_s_raw = keep("x_s_raw", [P, 2 * S], U8)
+        nc.vector.tensor_copy(x_s_raw[:, :S], xs_win[:].indirect(offs_t[:]))
+        nc.vector.tensor_copy(x_s_raw[:, S:], xs_win[:].indirect(two_t[:]))
+        for r in range(4):
+            nc.sync.dma_start(x_s[r:P:32, :].bitcast(I32), x_s_raw[2 * r : 32 : 8, :].bitcast(I32))
+        xq_s = x_s[:, :S]
+        x2_s = x_s[:, S:]
+        dw_win = placed("dw_win", [P, G], U32, 0)
+        nc.sync.dma_start(dw_win[:].bitcast(I32), d_words[0].rearrange("p c r -> p (c r)").bitcast(I32))
         dk_s_raw = stage.tile([P, H], U8, name="dk_s_raw", offset=0)
         nc.vector.tensor_copy(dk_s_raw[:], ds_win[:].indirect(k1_t[:]))
-        dk_s = deal("dk_s", dk_s_raw, U8, U8)
-        for e in range(2):
-            nc.sync.dma_start(dk_s[2 + e : P : 32, :].bitcast(I32), dk_s[16 + e : P : 32, :].bitcast(I32))
+        dk_s = deal("dk_s", dk_s_raw, U8, 2)
+        for r in range(1, 4):
+            nc.sync.dma_start(dk_s[r:P:32, :].bitcast(I32), dk_s[8 * r : P : 32, :].bitcast(I32))
 
-        w1_bf = keep("w1_bf", [P, PACK, P, PACK], BF16)
+        w1_bf = keep("w1_bf", [P, PACK, 16, 8, PACK], BF16)
         for u in range(2):
             nc.scalar.copy(
-                w1_bf[:, :, u * (P // 2) : (u + 1) * (P // 2), :].rearrange("p t m j -> p m j t"),
-                w1_raw[u][:].rearrange("p j (m t) -> p m j t", t=PACK),
+                w1_bf[:, :, 8 * u : 8 * u + 8, :, :].rearrange("p t b u j -> p b t u j"),
+                w1_raw[u][:].rearrange("p j (b t u) -> p b t u j", t=PACK, u=8),
             )
         w2_raw = stage.tile([P, PACK, N], F32, name="w2_raw", offset=0)
-        nc.sync.dma_start(w2_raw[:], w2.rearrange("(p j) c -> p j c", j=PACK))
+        w2_rows = w2.rearrange("(b t u) n -> t b u n", t=PACK, u=8)
+        for t in range(PACK):
+            nc.sync.dma_start(w2_raw[:, t, :], w2_rows[t])
         w1_q = keep("w1_q", [P, H], U32)
         w1_s = keep("w1_s", [P, H], U8)
-        nc.vector.quantize_mx(out=w1_q[:].bitcast(FP8X4), scales=w1_s[:], in_=w1_bf[:].rearrange("p t m j -> p (t m j)"))
+        nc.vector.quantize_mx(out=w1_q[:].bitcast(FP8X4), scales=w1_s[:], in_=w1_bf[:].rearrange("p t b u j -> p (t b u j)"))
         xq_w = pick("xq_w", xw_win, offs_t, U32)
 
         def product(lhs_q, lhs_s, t, rhs_q, rhs_s, dst):
@@ -126,19 +134,19 @@ def tile_picked_twkeyflowbratio_none_p_kernel(
         y_ps = []
         for t in range(PACK):
             bank = psum.tile([P, S], F32, name="bank")
-            product(w1_q, w1_s, t, xq_w[:], xq_s[:], bank[:])
+            product(w1_q, w1_s, t, xq_w[:], xq_s, bank[:])
             y_ps.append(bank)
 
         x2_w = pick("x2_w", xw_win, two_t, U32)
         dk_w_raw = pick("dk_w_raw", dw_win, k1_t, U32)
-        dk_w = deal("dk_w", dk_w_raw, U32, I32)
+        dk_w = deal("dk_w", dk_w_raw, U32, 8)
         d_ps = []
         for t in range(PACK):
             bank = psum.tile([P, S], F32, name="bank")
-            product(dk_w, dk_s, t, x2_w[:], x2_s[:], bank[:])
+            product(dk_w, dk_s, t, x2_w[:], x2_s, bank[:])
             d_ps.append(bank)
 
-        y_win = [placed("y_win2", [P, S], F32, 4) if t == 2 else keep("y_win%d" % t, [P, S], F32) for t in range(PACK)]
+        y_win = [keep("y_win0", [P, S], F32)] + [placed("y_win%d" % t, [P, S], F32, 2 * (t - 1)) for t in (1, 2, 3)]
         d_win = [keep("d_win%d" % t, [P, S], F32) for t in range(PACK)]
         h_win = [keep("h_win%d" % t, [P, S], F32) for t in range(PACK)]
         h_ps = [psum.tile([P, S], F32, name="bank") for t in range(PACK)]
@@ -146,47 +154,55 @@ def tile_picked_twkeyflowbratio_none_p_kernel(
         w2_s = keep("w2_s", [P, N], U8)
         gains = []
         for t in range(PACK):
-            g = work.tile([P, 1], F32, name="gain%d" % t, offset=GAIN_AT[t] * 1024, align_bytes=64)
-            nc.gpsimd.tensor_scalar(g[:], gain[:, t : t + 1], 0.0625, 0.0, ALU.mult, ALU.add)
+            g = placed("gain%d" % t, [P, 1], F32, GAIN_AT[t])
+            nc.gpsimd.dma_start(g[:], gn.rearrange("(b t u) o -> t b u o", t=PACK, u=8)[t])
             gains.append(g)
-        planes = [keep("planes%d" % half, [P, PACK, HALF], BF16) for half in range(2)]
+        planes = [keep("planes%d" % part, [P, PACK, hi - lo], BF16) for part, (lo, hi) in enumerate(PARTS)]
 
-        def fetch(t, half):
-            lc = slice(half * HALF // LANES, (half + 1) * HALF // LANES)
-            unit = half * PACK + t
-            diff = placed("got%d" % unit, [P, 2, HALF], F32, GOT_AT[unit])
-            nc.scalar.activation(diff[:, 0, :], y_win[t][:].indirect(n1_t[:, lc]), ACT.Copy)
-            nc.scalar.activation(diff[:, 1, :], y_win[t][:].indirect(n2_t[:, lc]), ACT.Copy)
-            return diff
+        def fetch(unit):
+            part, t = divmod(unit, PACK)
+            lo, hi = PARTS[part]
+            lc = slice(lo // LANES, hi // LANES)
+            got = placed("got%d" % unit, [P, 2, hi - lo], F32, GOT_AT[unit])
+            nc.scalar.activation(got[:, 0, :], y_win[t][:].indirect(n1_t[:, lc]), ACT.Copy)
+            nc.scalar.activation(got[:, 1, :], y_win[t][:].indirect(n2_t[:, lc]), ACT.Copy)
+            return got
 
-        def mix(t, half, diff):
-            cols = slice(half * HALF, (half + 1) * HALF)
-            lc = slice(half * HALF // LANES, (half + 1) * HALF // LANES)
-            unit = half * PACK + t
-            got = diff
-            diff = placed("diff%d" % unit, [P, 2, HALF], F32, DIFF_AT[unit])
+        def far_d(unit):
+            part, t = divmod(unit, PACK)
+            lo, hi = PARTS[part]
+            looked_up = d_win[t][:].indirect(n3_t[:, lo // LANES : hi // LANES])
+            if unit not in TRIPLE:
+                return looked_up
+            picked = placed("picked%d" % unit, [P, hi - lo], F32, 32 + 3 * (unit - 2))
+            nc.scalar.activation(picked[:], looked_up, ACT.Copy)
+            return picked[:]
+
+        def mix(unit, got, d_far):
+            part, t = divmod(unit, PACK)
+            lo, hi = PARTS[part]
+            diff = placed("diff%d" % unit, [P, 2, hi - lo], F32, DIFF_AT[unit % 2])
             nc.vector.tensor_tensor(
-                diff[:], got[:], y_win[t][:, cols].unsqueeze(1).broadcast_to([P, 2, HALF]), ALU.subtract
+                diff[:], got[:], y_win[t][:, lo:hi].unsqueeze(1).broadcast_to([P, 2, hi - lo]), ALU.subtract
             )
-            far = placed("far%d" % unit, [P, HALF], F32, 20 + 2 * unit)
-            nc.vector.tensor_tensor(far[:], d_win[t][:].indirect(n3_t[:, lc]), diff[:, 1, :], ALU.mult)
-            near = placed("near%d" % unit, [P, HALF], F32, 21 + 2 * unit)
-            nc.vector.tensor_tensor(near[:], diff[:, 0, :], d_win[t][:, cols], ALU.mult)
-            nc.vector.scalar_tensor_tensor(planes[half][:, t, :], far[:], 0.5, near[:], ALU.mult, ALU.add)
+            terms = placed("terms%d" % unit, [P, 2, hi - lo], F32, 32 + 3 * unit)
+            nc.vector.tensor_tensor(terms[:, 1, :], d_far, diff[:, 1, :], ALU.mult)
+            nc.vector.scalar_tensor_tensor(terms[:, 0, :], diff[:, 0, :], 0.0625, d_win[t][:, lo:hi], ALU.mult, ALU.mult)
+            nc.vector.scalar_tensor_tensor(planes[part][:, t, :], terms[:, 1, :], 0.03125, terms[:, 0, :], ALU.mult, ALU.add)
 
         def y_out(t):
-            copy = nc.vector.tensor_copy if t == 2 else nc.scalar.copy
+            copy = nc.vector.tensor_copy if t == 1 else nc.scalar.copy
             copy(y_win[t][:], y_ps[t][:])
 
         def d_out(t):
-            if t < 1:
+            if t == 0:
                 nc.vector.tensor_scalar(d_win[t][:], d_ps[t][:], gains[t][:], None, ALU.mult)
             else:
                 nc.scalar.activation(d_win[t][:], d_ps[t][:], ACT.Copy, scale=gains[t][:])
 
         def w2_round(u):
             cols = slice(u * (N // 2), (u + 1) * (N // 2))
-            w2_bf = placed("w2_bf%d" % u, [P, N // 2, PACK], BF16, 20 + 2 * (2 + u))
+            w2_bf = placed("w2_bf%d" % u, [P, N // 2, PACK], BF16, 32 + 3 * (1 + u))
             nc.scalar.copy(
                 w2_bf[:].rearrange("p (c i) j -> p c j i", i=4),
                 w2_raw[:, :, cols].rearrange("p j (c i) -> p c j i", i=4),
@@ -195,52 +211,41 @@ def tile_picked_twkeyflowbratio_none_p_kernel(
                 out=w2_q[:, cols].bitcast(FP8X4), scales=w2_s[:, cols], in_=w2_bf[:].rearrange("p n j -> p (n j)")
             )
 
-        z_bf = [keep("z_bf%d" % half, [P, HALF, PACK], BF16) for half in range(2)]
-
-        def weave(half, copy, lo, hi):
-            copy(
-                z_bf[half][:, lo:hi, :].rearrange("p (c i) t -> p c t i", i=4),
-                planes[half][:, :, lo:hi].rearrange("p t (c i) -> p c t i", i=4),
-            )
-
-        def last_product(half, by_vector):
-            cols = slice(half * HALF, (half + 1) * HALF)
-            z_q = keep("z_q%d" % half, [P, HALF], U32)
-            z_s = keep("z_s%d" % half, [P, HALF], U8)
-            nc.vector.quantize_mx(out=z_q[:].bitcast(FP8X4), scales=z_s[:], in_=z_bf[half][:].rearrange("p n t -> p (n t)"))
+        def last_product(part, weave, by_vector):
+            lo, hi = PARTS[part]
+            z_bf = keep("z_bf%d" % part, [P, hi - lo, PACK], BF16)
+            weave(z_bf[:].rearrange("p (c i) t -> p c t i", i=4), planes[part][:].rearrange("p t (c i) -> p c t i", i=4))
+            z_q = keep("z_q%d" % part, [P, hi - lo], U32)
+            z_s = keep("z_s%d" % part, [P, hi - lo], U8)
+            nc.vector.quantize_mx(out=z_q[:].bitcast(FP8X4), scales=z_s[:], in_=z_bf[:].rearrange("p n t -> p (n t)"))
             for t in range(PACK):
-                product(w2_q, w2_s, t, z_q[:], z_s[:], h_ps[t][:, cols])
-                if t in by_vector:
-                    nc.vector.tensor_copy(h_win[t][:, cols], h_ps[t][:, cols])
-                else:
-                    nc.scalar.copy(h_win[t][:, cols], h_ps[t][:, cols])
+                for c0 in range(lo, hi, 256):
+                    c1 = min(c0 + 256, hi)
+                    product(w2_q, w2_s, t, z_q[:, c0 - lo : c1 - lo], z_s[:, c0 - lo : c1 - lo], h_ps[t][:, c0:c1])
+                copy = nc.vector.tensor_copy if t in by_vector else nc.scalar.copy
+                copy(h_win[t][:, lo:hi], h_ps[t][:, lo:hi])
 
         y_out(0)
+        got = [fetch(0)]
         y_out(1)
-        got = [fetch(0, 0)]
         y_out(2)
-        got.append(fetch(1, 0))
+        got.append(fetch(1))
         y_out(3)
         for unit in range(2 * PACK):
-            half, t = divmod(unit, PACK)
-            if half == 0:
-                d_out(t)
-            mix(t, half, got[unit])
+            if unit < PACK:
+                d_out(unit)
+            mix(unit, got[unit], far_d(unit))
             if unit + 2 < 2 * PACK:
-                got.append(fetch((unit + 2) % PACK, (unit + 2) // PACK))
-            if unit == 4:
+                got.append(fetch(unit + 2))
+            if unit == 3:
                 w2_round(0)
-            if unit == 5:
+            if unit == 4:
                 w2_round(1)
-                weave(0, nc.scalar.copy, 0, HALF)
-            if unit == 6:
-                last_product(0, ())
-        weave(1, nc.vector.tensor_copy, 0, 160)
-        weave(1, nc.scalar.copy, 160, HALF)
-        last_product(1, (1, 3))
-
-        size = [placed("size%d" % u, [P, 2, W], F32, (36, 40)[u]) for u in range(2)]
-        res = [placed("res%d" % t, [P, S], F32, (39, 44, 41, 46)[t]) for t in range(PACK)]
+            if unit == 5:
+                last_product(0, nc.scalar.copy, ())
+        last_product(1, nc.vector.tensor_copy, (1, 3))
+        size = [placed("size%d" % u, [P, 2, W], F32, (60, 64)[u]) for u in range(2)]
+        res = [placed("res%d" % t, [P, S], F32, (63, 68, 65, 70)[t]) for t in range(PACK)]
         pa = keep("pa", [P, PACK, W], F32)
         pb = keep("pb", [P, PACK, W], F32)
         root = keep("root", [P, PACK, W], F32)

@@ -202,7 +202,7 @@ def tile_picked_twkeyflowbratio_none_p_kernel(
 
         def w2_round(u):
             cols = slice(u * (N // 2), (u + 1) * (N // 2))
-            w2_bf = placed("w2_bf%d" % u, [P, N // 2, PACK], BF16, 32 + 3 * (1 + u))
+            w2_bf = placed("w2_bf%d" % u, [P, N // 2, PACK], BF16, 32 + 3 * (2 + u))
             nc.scalar.copy(
                 w2_bf[:].rearrange("p (c i) j -> p c j i", i=4),
                 w2_raw[:, :, cols].rearrange("p j (c i) -> p c j i", i=4),
@@ -211,14 +211,18 @@ def tile_picked_twkeyflowbratio_none_p_kernel(
                 out=w2_q[:, cols].bitcast(FP8X4), scales=w2_s[:, cols], in_=w2_bf[:].rearrange("p n j -> p (n j)")
             )
 
-        def last_product(part, weave, by_vector):
+        def z_quantise(part, weave):
             lo, hi = PARTS[part]
             z_bf = keep("z_bf%d" % part, [P, hi - lo, PACK], BF16)
             weave(z_bf[:].rearrange("p (c i) t -> p c t i", i=4), planes[part][:].rearrange("p t (c i) -> p c t i", i=4))
             z_q = keep("z_q%d" % part, [P, hi - lo], U32)
             z_s = keep("z_s%d" % part, [P, hi - lo], U8)
             nc.vector.quantize_mx(out=z_q[:].bitcast(FP8X4), scales=z_s[:], in_=z_bf[:].rearrange("p n t -> p (n t)"))
-            for t in range(PACK):
+            return z_q, z_s
+
+        def last_product(part, z_q, z_s, tiles, by_vector):
+            lo, hi = PARTS[part]
+            for t in tiles:
                 for c0 in range(lo, hi, 256):
                     c1 = min(c0 + 256, hi)
                     product(w2_q, w2_s, t, z_q[:, c0 - lo : c1 - lo], z_s[:, c0 - lo : c1 - lo], h_ps[t][:, c0:c1])
@@ -240,10 +244,11 @@ def tile_picked_twkeyflowbratio_none_p_kernel(
             if unit == 3:
                 w2_round(0)
             if unit == 4:
-                w2_round(1)
+                z_first = z_quantise(0, nc.scalar.copy)
             if unit == 5:
-                last_product(0, nc.scalar.copy, ())
-        last_product(1, nc.vector.tensor_copy, (1, 3))
+                w2_round(1)
+                last_product(0, *z_first, range(PACK), ())
+        last_product(1, *z_quantise(1, nc.vector.tensor_copy), range(PACK), (1, 3))
         size = [placed("size%d" % u, [P, 2, W], F32, (60, 64)[u]) for u in range(2)]
         res = [placed("res%d" % t, [P, S], F32, (63, 68, 65, 70)[t]) for t in range(PACK)]
         pa = keep("pa", [P, PACK, W], F32)

from contextlib import ExitStack

import concourse.mybir as mybir

K, T, S, N, H, G, W = 512, 2048, 512, 512, 512, 2048, 256
FLOPS = 2 * (K * H * S + K * H * S + H * N * S)

F32 = mybir.dt.float32
BF16 = mybir.dt.bfloat16
I32 = mybir.dt.int32
U32 = mybir.dt.uint32
U16 = mybir.dt.uint16
U8 = mybir.dt.uint8
FP8X4 = mybir.dt.float8_e4m3fn_x4
ALU = mybir.AluOpType
ACT = mybir.ActivationFunctionType

P = 128
PACK = 4
HALF = S // 2
LANES = 16
PARTS = ((0, 384), (384, 512))
TRIPLE = (3,)
GOT_AT = (14, 22, 15, 23, 16, 23, 16, 23)
DIFF_AT = (6, 10)
GAIN_AT = (10, 17, 25, 18)


def tile_picked_twkeyflowbratio_none_p_kernel(
    tc, x_words, x_scales, w1, d_words, d_scales, gn, w2, offs, k1, two, n1, n2, n3, n4, n5, out
):
    nc = tc.nc
    with ExitStack() as ctx:
        held = ctx.enter_context(tc.tile_pool(name="held", bufs=1))
        stage = ctx.enter_context(tc.tile_pool(name="stage", bufs=1))
        work = ctx.enter_context(tc.tile_pool(name="work", bufs=1))
        psum = ctx.enter_context(tc.psum_pool(name="psum", bufs=8))

        def keep(name, shape, dtype):
            return held.tile(shape, dtype, name=name, align_bytes=64)

        def placed(name, shape, dtype, at):
            return work.tile(shape, dtype, name=name, offset=at * 1024, align_bytes=64)

        def load_list(name, src):
            t = held.tile(list(src.shape), U16, name=name)
            nc.sync.dma_start(t[:], src)
            return t

        xs_win = placed("xs_win", [P, T], U8, 0)
        ds_win = keep("ds_win", [P, G], U8)
        x_s = keep("x_s", [P, 2 * S], U8)
        nc.gpsimd.memset(x_s[:].bitcast(I32), 0)
        warm = keep("warm", [P, 8], F32)
        nc.gpsimd.memset(warm[:], 1.0)
        nc.scalar.activation(warm[:], warm[:], ACT.Abs_reciprocal_sqrt, bias=0.5)

        def load_scales(window, scales):
            nc.sync.dma_start(window[:].bitcast(I32), scales[0].bitcast(I32).unsqueeze(1).broadcast_to([16, 8, T // 4]))

        offs_t = load_list("offs_t", offs)
        nc.sync.dma_start(
            xs_win[:32, :].bitcast(I32), x_scales[0].bitcast(I32).unsqueeze(1).broadcast_to([16, 2, T // 4])
        )
        nc.vector.memset(xs_win[32:64, :].bitcast(I32), 0)
        nc.vector.memset(xs_win[64:, :].bitcast(I32), 0)
        two_t = load_list("two_t", two)
        k1_t = load_list("k1_t", k1)
        load_scales(ds_win, d_scales)
        n1_t = load_list("n1_t", n1)
        n2_t = load_list("n2_t", n2)
        w1_rows = w1.rearrange("(p j) c -> p j c", j=PACK)
        w1_raw = []
        for u in range(2):
            raw = stage.tile([P, PACK, H // 2], F32, name="w1_raw%d" % u, offset=H + u * PACK * (H // 2) * 4)
            nc.sync.dma_start(raw[:], w1_rows[:, :, u * (H // 2) : (u + 1) * (H // 2)])
            w1_raw.append(raw)
        n3_t = load_list("n3_t", n3)
        n4_t = load_list("n4_t", n4)
        n5_t = load_list("n5_t", n5)
        xw_win = keep("xw_win", [P, T], U32)
        nc.sync.dma_start(xw_win[:].bitcast(I32), x_words[0].rearrange("p c r -> p (c r)").bitcast(I32))

        def pick(name, window, offsets, dtype):
            t = keep(name, [P, S], dtype)
            nc.vector.tensor_copy(t[:], window[:].indirect(offsets[:]))
            return t

        def deal(name, src, dtype, run):
            t = keep(name, [P, H], dtype)
            nc.vector.tensor_copy(
                t[:].bitcast(I32).rearrange("p (t b u) -> p t b u", t=PACK, u=run),
                src[:].bitcast(I32).rearrange("p (b t u) -> p t b u", t=PACK, u=run),
            )
            return t

        x_s_raw = keep("x_s_raw", [P, 2 * S], U8)
        nc.vector.tensor_copy(x_s_raw[:, :S], xs_win[:].indirect(offs_t[:]))
        nc.vector.tensor_copy(x_s_raw[:, S:], xs_win[:].indirect(two_t[:]))
        for r in range(4):
            nc.sync.dma_start(x_s[r:P:32, :].bitcast(I32), x_s_raw[2 * r : 32 : 8, :].bitcast(I32))
        xq_s = x_s[:, :S]
        x2_s = x_s[:, S:]
        dw_win = placed("dw_win", [P, G], U32, 0)
        nc.sync.dma_start(dw_win[:].bitcast(I32), d_words[0].rearrange("p c r -> p (c r)").bitcast(I32))
        dk_s_raw = stage.tile([P, H], U8, name="dk_s_raw", offset=0)
        nc.vector.tensor_copy(dk_s_raw[:], ds_win[:].indirect(k1_t[:]))
        dk_s = deal("dk_s", dk_s_raw, U8, 2)
        for r in range(1, 4):
            nc.sync.dma_start(dk_s[r:P:32, :].bitcast(I32), dk_s[8 * r : P : 32, :].bitcast(I32))

        w1_bf = keep("w1_bf", [P, PACK, 16, 8, PACK], BF16)
        for u in range(2):
            nc.scalar.copy(
                w1_bf[:, :, 8 * u : 8 * u + 8, :, :].rearrange("p t b u j -> p b t u j"),
                w1_raw[u][:].rearrange("p j (b t u) -> p b t u j", t=PACK, u=8),
            )
        w2_raw = stage.tile([P, PACK, N], F32, name="w2_raw", offset=0)
        w2_rows = w2.rearrange("(b t u) n -> t b u n", t=PACK, u=8)
        for t in range(PACK):
            nc.sync.dma_start(w2_raw[:, t, :], w2_rows[t])
        w1_q = keep("w1_q", [P, H], U32)
        w1_s = keep("w1_s", [P, H], U8)
        nc.vector.quantize_mx(out=w1_q[:].bitcast(FP8X4), scales=w1_s[:], in_=w1_bf[:].rearrange("p t b u j -> p (t b u j)"))
        xq_w = pick("xq_w", xw_win, offs_t, U32)

        def product(lhs_q, lhs_s, t, rhs_q, rhs_s, dst):
            cols = slice(t * P, (t + 1) * P)
            nc.tensor.matmul_mx(
                out=dst, lhsT=lhs_q[:, cols].bitcast(FP8X4), lhsT_scale=lhs_s[:, cols],
                rhs=rhs_q.bitcast(FP8X4), rhs_scale=rhs_s, start=True, stop=True,
            )

        y_ps = []
        for t in range(PACK):
            bank = psum.tile([P, S], F32, name="bank")
            product(w1_q, w1_s, t, xq_w[:], xq_s, bank[:])
            y_ps.append(bank)

        x2_w = pick("x2_w", xw_win, two_t, U32)
        dk_w_raw = pick("dk_w_raw", dw_win, k1_t, U32)
        dk_w = deal("dk_w", dk_w_raw, U32, 8)
        d_ps = []
        for t in range(PACK):
            bank = psum.tile([P, S], F32, name="bank")
            product(dk_w, dk_s, t, x2_w[:], x2_s, bank[:])
            d_ps.append(bank)

        y_win = [keep("y_win0", [P, S], F32)] + [placed("y_win%d" % t, [P, S], F32, 2 * (t - 1)) for t in (1, 2, 3)]
        d_win = [keep("d_win%d" % t, [P, S], F32) for t in range(PACK)]
        h_win = [keep("h_win%d" % t, [P, S], F32) for t in range(PACK)]
        h_ps = [psum.tile([P, S], F32, name="bank") for t in range(PACK)]
        w2_q = keep("w2_q", [P, N], U32)
        w2_s = keep("w2_s", [P, N], U8)
        gains = []
        for t in range(PACK):
            g = placed("gain%d" % t, [P, 1], F32, GAIN_AT[t])
            nc.gpsimd.dma_start(g[:], gn.rearrange("(b t u) o -> t b u o", t=PACK, u=8)[t])
            gains.append(g)
        planes = [keep("planes%d" % part, [P, PACK, hi - lo], BF16) for part, (lo, hi) in enumerate(PARTS)]

        def fetch(unit):
            part, t = divmod(unit, PACK)
            lo, hi = PARTS[part]
            lc = slice(lo // LANES, hi // LANES)
            got = placed("got%d" % unit, [P, 2, hi - lo], F32, GOT_AT[unit])
            nc.scalar.activation(got[:, 0, :], y_win[t][:].indirect(n1_t[:, lc]), ACT.Copy)
            nc.scalar.activation(got[:, 1, :], y_win[t][:].indirect(n2_t[:, lc]), ACT.Copy)
            return got

        def far_d(unit):
            part, t = divmod(unit, PACK)
            lo, hi = PARTS[part]
            looked_up = d_win[t][:].indirect(n3_t[:, lo // LANES : hi // LANES])
            if unit not in TRIPLE:
                return looked_up
            picked = placed("picked%d" % unit, [P, hi - lo], F32, 32 + 3 * (unit - 2))
            nc.scalar.activation(picked[:], looked_up, ACT.Copy)
            return picked[:]

        def mix(unit, got, d_far):
            part, t = divmod(unit, PACK)
            lo, hi = PARTS[part]
            diff = placed("diff%d" % unit, [P, 2, hi - lo], F32, DIFF_AT[unit % 2])
            nc.vector.tensor_tensor(
                diff[:], got[:], y_win[t][:, lo:hi].unsqueeze(1).broadcast_to([P, 2, hi - lo]), ALU.subtract
            )
            terms = placed("terms%d" % unit, [P, 2, hi - lo], F32, 32 + 3 * unit)
            nc.vector.tensor_tensor(terms[:, 1, :], d_far, diff[:, 1, :], ALU.mult)
            nc.vector.scalar_tensor_tensor(terms[:, 0, :], diff[:, 0, :], 0.0625, d_win[t][:, lo:hi], ALU.mult, ALU.mult)
            nc.vector.scalar_tensor_tensor(planes[part][:, t, :], terms[:, 1, :], 0.03125, terms[:, 0, :], ALU.mult, ALU.add)

        def y_out(t):
            copy = nc.vector.tensor_copy if t == 1 else nc.scalar.copy
            copy(y_win[t][:], y_ps[t][:])

        def d_out(t):
            if t == 0:
                nc.vector.tensor_scalar(d_win[t][:], d_ps[t][:], gains[t][:], None, ALU.mult)
            else:
                nc.scalar.activation(d_win[t][:], d_ps[t][:], ACT.Copy, scale=gains[t][:])

        def w2_round(u):
            cols = slice(u * (N // 2), (u + 1) * (N // 2))
            w2_bf = placed("w2_bf%d" % u, [P, N // 2, PACK], BF16, 32 + 3 * (2 + u))
            nc.scalar.copy(
                w2_bf[:].rearrange("p (c i) j -> p c j i", i=4),
                w2_raw[:, :, cols].rearrange("p j (c i) -> p c j i", i=4),
            )
            nc.vector.quantize_mx(
                out=w2_q[:, cols].bitcast(FP8X4), scales=w2_s[:, cols], in_=w2_bf[:].rearrange("p n j -> p (n j)")
            )

        def z_quantise(part, weave):
            lo, hi = PARTS[part]
            z_bf = keep("z_bf%d" % part, [P, hi - lo, PACK], BF16)
            weave(z_bf[:].rearrange("p (c i) t -> p c t i", i=4), planes[part][:].rearrange("p t (c i) -> p c t i", i=4))
            z_q = keep("z_q%d" % part, [P, hi - lo], U32)
            z_s = keep("z_s%d" % part, [P, hi - lo], U8)
            nc.vector.quantize_mx(out=z_q[:].bitcast(FP8X4), scales=z_s[:], in_=z_bf[:].rearrange("p n t -> p (n t)"))
            return z_q, z_s

        def last_product(part, z_q, z_s, tiles, by_vector):
            lo, hi = PARTS[part]
            for t in tiles:
                for c0 in range(lo, hi, 256):
                    c1 = min(c0 + 256, hi)
                    product(w2_q, w2_s, t, z_q[:, c0 - lo : c1 - lo], z_s[:, c0 - lo : c1 - lo], h_ps[t][:, c0:c1])
                copy = nc.vector.tensor_copy if t in by_vector else nc.scalar.copy
                copy(h_win[t][:, lo:hi], h_ps[t][:, lo:hi])

        y_out(0)
        got = [fetch(0)]
        y_out(1)
        y_out(2)
        got.append(fetch(1))
        y_out(3)
        for unit in range(2 * PACK):
            if unit < PACK:
                d_out(unit)
            mix(unit, got[unit], far_d(unit))
            if unit + 2 < 2 * PACK:
                got.append(fetch(unit + 2))
            if unit == 3:
                w2_round(0)
            if unit == 4:
                z_first = z_quantise(0, nc.scalar.copy)
            if unit == 5:
                w2_round(1)
                last_product(0, *z_first, range(PACK), ())
        last_product(1, *z_quantise(1, nc.vector.tensor_copy), range(PACK), (1, 3))
        size = [placed("size%d" % u, [P, 2, W], F32, (60, 64)[u]) for u in range(2)]
        res = [placed("res%d" % t, [P, S], F32, (63, 68, 65, 70)[t]) for t in range(PACK)]
        pa = keep("pa", [P, PACK, W], F32)
        pb = keep("pb", [P, PACK, W], F32)
        root = keep("root", [P, PACK, W], F32)
        larger = keep("larger", [P, PACK, W], F32)
        part = keep("part", [P, PACK, W], F32)
        pairs = (slice(0, 2), slice(2, 4))

        for t in range(PACK):
            nc.vector.tensor_copy(pa[:, t, :], h_win[t][:].indirect(n4_t[:]))
            nc.scalar.activation(pb[:, t, :], h_win[t][:].indirect(n5_t[:]), ACT.Copy)
        for u, pair in enumerate(pairs):
            nc.scalar.activation(size[u][:], pb[:, pair, :], ACT.Abs)
            nc.vector.tensor_tensor(larger[:, pair, :], pa[:, pair, :], pb[:, pair, :], ALU.max)
        for u, pair in enumerate(pairs):
            nc.scalar.activation(root[:, pair, :], size[u][:], ACT.Abs_reciprocal_sqrt, bias=0.5)
            nc.vector.tensor_tensor(part[:, pair, :], pa[:, pair, :], root[:, pair, :], ALU.mult)

        def put_larger(t):
            nc.scalar.activation(res[t][:].indirect(n5_t[:]), larger[:, t, :], ACT.Copy)

        def put_ratio(t):
            nc.vector.tensor_tensor(res[t][:].indirect(n4_t[:]), part[:, t, :], root[:, t, :], ALU.mult)

        for t in (0, 2):
            put_larger(t)
            put_ratio(t + 1)
        for t in (0, 2):
            put_larger(t + 1)
            put_ratio(t)
            nc.sync.dma_start(out[(t + 1) * P : (t + 2) * P, :], res[t + 1][:])
            nc.sync.dma_start(out[t * P : (t + 1) * P, :], res[t][:])
